import numpy as np
import ml_dtypes


def mxq(x, axis, fmt="e4m3"):
    dtype, down = {"e4m3": (ml_dtypes.float8_e4m3fn, 7), "e5m2": (ml_dtypes.float8_e5m2, 14)}[fmt]
    v = np.moveaxis(np.asarray(x, np.float32).astype(ml_dtypes.bfloat16).astype(np.float64), axis, -1)
    blocks = v.reshape(v.shape[:-1] + (-1, 32))
    amax = np.abs(blocks).max(-1, keepdims=True)
    byte = np.maximum(np.where(amax > 0, np.frexp(amax)[1] - 1 + 127, 0) - down, 1)
    scale = np.exp2(byte - 127.0)
    codes = (blocks / scale).astype(np.float32).astype(dtype).astype(np.float64)
    return np.moveaxis((codes * scale).reshape(v.shape), -1, axis)


WIDE = False


def mx_kscale(k):
    if not WIDE:
        return np.ones(k)
    levels = np.array([10, -10, 5, -5, 0])
    if k % 512:
        return np.exp2(np.random.permutation(np.resize(levels, k // 32))).repeat(32)
    a = np.empty((k // 512, 16))
    for p in range(k // 512):
        a[p, :8] = np.random.permutation(np.resize(levels, 8))
        for g in range(8):
            far = levels[np.abs(levels - a[p, g]) >= 10]
            a[p, g + 8] = far[np.random.randint(len(far))]
    return np.exp2(a.ravel()).repeat(32)


def f64(x):
    return np.asarray(x).astype(np.float64)


def striped(idx):
    return np.tile(idx.reshape(-1, 16).T, (8, 1)).astype(np.uint16)


def unstriped(offs):
    return offs[:16].T.reshape(-1).astype(np.int64)


E2M1 = np.array([0.0, 0.5, 1.0, 1.5, 2.0, 3.0, 4.0, 6.0, -0.0, -0.5, -1.0, -1.5, -2.0, -3.0, -4.0, -6.0])


def pack_weight(w, fmt):
    k, n = w.shape
    w = f64(np.asarray(w, np.float32).astype(ml_dtypes.bfloat16)).reshape(k // 32, 32, n)
    amax = np.abs(w).max(1)
    if fmt == "e4m3":
        byte = np.frexp(amax)[1] - 1 + 127 - 7
    else:
        mant, ex = np.frexp(amax / 6.0)
        byte = np.where(mant > 0.5, ex, ex - 1) + 127
    byte = np.clip(np.where(amax > 0, byte, 1), 1, 254)
    scaled = (w * np.exp2(127.0 - byte)[:, None, :]).reshape(k, n).astype(np.float32)
    by_word = np.ascontiguousarray(scaled.reshape(k // 512, 128, 4, n).transpose(0, 1, 3, 2))
    if fmt == "e4m3":
        words = by_word.astype(ml_dtypes.float8_e4m3fn).view(np.uint8)
    else:
        c = by_word.astype(ml_dtypes.float4_e2m1fn).view(np.uint8) & 0xF
        words = (c[..., 0::2] | (c[..., 1::2] << 4)).reshape(k // 512, 128, 2 * n)
    return np.ascontiguousarray(words), np.ascontiguousarray(byte.astype(np.uint8).reshape(k // 512, 16, n))


def unpack_weight(words, scales, fmt):
    g, _, n = scales.shape
    words = np.ascontiguousarray(words).reshape(g, 128, n, -1)
    if fmt == "e4m3":
        vals = words.view(ml_dtypes.float8_e4m3fn).astype(np.float64)
    else:
        nib = np.empty((g, 128, n, 4), np.uint8)
        nib[..., 0::2] = words & 0xF
        nib[..., 1::2] = words >> 4
        vals = E2M1[nib]
    vals = vals * np.repeat(np.exp2(scales.astype(np.float64) - 127.0), 8, axis=1)[..., None]
    return vals.transpose(0, 1, 3, 2).reshape(g * 512, n)


K, T, E, C, N = 2560, 384, 12, 128, 256
TOP = 4
K8 = 1024


def by_expert(wq, xq):
    return np.concatenate([wq[e].T @ xq[:, e * C:(e + 1) * C] for e in range(E)], axis=1)


def setup_inputs():
    n = np.random.standard_normal
    s = mx_kscale(K)[:, None]
    deal = np.repeat(np.arange(E), C).reshape(TOP, T)[:, np.random.permutation(T)]
    deal = np.take_along_axis(deal, np.argsort(np.random.rand(TOP, T), axis=0), axis=0)
    for _ in range(8):
        s_, t_ = np.random.permutation(T).reshape(2, -1); r = np.random.randint(TOP, size=T // 2); x, y = deal[r, s_].copy(), deal[r, t_].copy()
        ok = ~((deal[:, s_] == y).any(0) | (deal[:, t_] == x).any(0)); deal[r[ok], s_[ok]] = y[ok]; deal[r[ok], t_[ok]] = x[ok]
    order = np.lexsort((np.random.rand(TOP * T), deal.reshape(-1)))
    slot_token = order % T; pos = np.empty(TOP * T, np.int64); pos[order] = np.arange(TOP * T); pos = pos.reshape(TOP, T)
    g = np.random.uniform(0.5, 1.5, (TOP, T)); g = g / g.sum(0)
    w = n((E, K, N)) / np.sqrt(K) / s[None]
    w8 = [pack_weight(m[:K8], "e4m3") for m in w]
    w4 = [pack_weight(m[K8:], "e2m1") for m in w]
    return {
        "xT": (n((K, T)) * s).astype(np.float32),
        "w8_words": np.stack([m[0] for m in w8]),
        "w8_scales": np.stack([m[1] for m in w8]),
        "w4_words": np.stack([m[0] for m in w4]),
        "w4_scales": np.stack([m[1] for m in w4]),
        "gate": np.stack([np.tile(r, (N, 1)) for r in g]).astype(np.float32),
        "offs": striped(slot_token),
        "pos1": striped(pos[0]),
        "pos2": striped(pos[1]),
        "pos3": striped(pos[2]),
        "pos4": striped(pos[3]),
    }


def reference(xT, w8_words, w8_scales, w4_words, w4_scales, gate, offs, pos1, pos2, pos3, pos4):
    idx = unstriped(offs)
    w = np.stack([np.concatenate([unpack_weight(w8_words[e], w8_scales[e], "e4m3"), unpack_weight(w4_words[e], w4_scales[e], "e2m1")]) for e in range(E)])
    xq = mxq(f64(xT)[:, idx], 0, "e4m3")
    y = by_expert(w, xq)
    return sum(f64(gate[r]) * y[:, unstriped(p)] for r, p in enumerate((pos1, pos2, pos3, pos4)))

@@ -1,0 +1,247 @@
+from contextlib import ExitStack
+
+import concourse.mybir as mybir
+
+F32 = mybir.dt.float32
+BF16 = mybir.dt.bfloat16
+I32 = mybir.dt.int32
+U32 = mybir.dt.uint32
+U16 = mybir.dt.uint16
+U8 = mybir.dt.uint8
+FP8X4 = mybir.dt.float8_e4m3fn_x4
+FP4X4 = mybir.dt.float4_e2m1fn_x4
+COPY = mybir.ActivationFunctionType.Copy
+MULT = mybir.AluOpType.mult
+ADD = mybir.AluOpType.add
+
+P = 128
+K, T, E, C, N = 2560, 384, 12, 128, 256
+TOP = 4
+SLOTS = E * C
+PASSES = 5
+PASSES8 = 2
+PASSES4 = 3
+HALVES = N // P
+GROUP = 384
+GROUPS = SLOTS // GROUP
+W_EXPERTS = E // GROUPS
+WINDOW = 512
+FLOPS = 2 * SLOTS * K * N
+
+ROW = {2: 0, 0: 4, 1: 8, 3: 12, 4: 16}
+SUM_ORDER = (2, 0, 4, 3, 1)
+MOVED_ROWS = 112
+W8_BYTES = PASSES8 * 4 * N
+W4_BYTES = PASSES4 * 2 * N
+
+
+def tile_moe_tk_lin_none_kernel(
+    tc, xT, w8_words, w8_scales, w4_words, w4_scales, gate, offs, pos1, pos2, pos3, pos4, out
+):
+    nc = tc.nc
+    with ExitStack() as ctx:
+        keep = ctx.enter_context(tc.tile_pool(name="keep", bufs=1))
+        psum = ctx.enter_context(tc.psum_pool(name="psum", bufs=8))
+
+        def tile(shape, dtype, name, tag=""):
+            return keep.tile(shape, dtype, name=name, tag=tag or name, align_bytes=64)
+
+        offs_list = keep.tile([P, SLOTS // 16], U16, name="offs_list")
+        pos_lists = [keep.tile([P, T // 16], U16, name="pos%d_list" % r) for r in range(TOP)]
+
+        slot = {3: "slot_a", 2: "slot_b"}
+        raw = [tile([P, 4, T], F32, "raw%d" % a, slot.get(a, "")) for a in range(PASSES)]
+        big = [tile([P, 256, 4], BF16, "big%d" % a) for a in range(PASSES)]
+        small = [tile([P, 128, 4], BF16, "small%d" % a) for a in range(PASSES)]
+        codes = [tile([P, WINDOW], U32, "codes%d" % a) for a in range(PASSES)]
+        words = [tile([P, SLOTS], U32, "words%d" % a) for a in range(PASSES)]
+        planes_a = tile([P, T], U8, "planes_a", "slot_c")
+        planes_b = tile([P, T], U8, "planes_b")
+        planes = tile([P, WINDOW], U8, "planes", "slot_d")
+        bytes_g = tile([P, SLOTS], U8, "bytes_g")
+        moved = {a: tile([P, SLOTS], U8, "moved%d" % a) for a in (3, 4)}
+        s8 = tile([P, E * PASSES8, N], U8, "s8")
+        s4 = tile([P, E * PASSES4, N], U8, "s4")
+        y = [tile([P, SLOTS], F32, "y%d" % h) for h in range(HALVES)]
+        prod = [tile([P, TOP, T], F32, "prod%d" % h) for h in range(HALVES)]
+        part = [tile([P, 2, T], F32, "part%d" % h) for h in range(HALVES)]
+        res = [tile([P, T], F32, "res%d" % h) for h in range(HALVES)]
+
+        def load_x(a, lo, hi):
+            rows = xT[512 * a : 512 * (a + 1), :].rearrange("(p j) w -> p j w", j=4)
+            nc.sync.dma_start(raw[a][:, :, lo:hi], rows[:, :, lo:hi])
+
+        def load_scales(scales, dram):
+            rows = dram.rearrange("e a (q r) n -> q r (e a) n", r=4)
+            for q in range(4):
+                nc.gpsimd.dma_start(scales[32 * q : 32 * q + 4, :, :].bitcast(I32), rows[q].bitcast(I32))
+
+        def load_weights(g, slot_name):
+            w = tile([P, W_EXPERTS * (W8_BYTES + W4_BYTES)], U8, "w%d" % g, slot_name)
+            ee = slice(W_EXPERTS * g, W_EXPERTS * (g + 1))
+            w8 = w[:, 0 : W_EXPERTS * W8_BYTES].rearrange("p (ea b) -> p ea b", b=4 * N)
+            w4 = w[:, W_EXPERTS * W8_BYTES :].rearrange("p (ea b) -> p ea b", b=2 * N)
+            nc.sync.dma_start(w8.bitcast(I32), w8_words[ee].rearrange("e a p n r -> p (e a) (n r)").bitcast(I32))
+            nc.sync.dma_start(w4.bitcast(I32), w4_words[ee].rearrange("e a p b -> p (e a) b").bitcast(I32))
+            return w8, w4
+
+        def turn(dst, a, lo, hi, on_vector):
+            src = raw[a][:, :, lo:hi].rearrange("p j w -> p w j")
+            if on_vector:
+                nc.vector.tensor_copy(out=dst[:], in_=src)
+            else:
+                nc.scalar.activation(dst[:], src, COPY)
+
+        def turn_all(a, big_v=False, small_v=False):
+            turn(big[a], a, 0, 256, big_v)
+            turn(small[a], a, 256, T, small_v)
+
+        def quantise(a):
+            row = min(ROW[a], 12)
+            plane = planes_b if a == 4 else planes_a
+            for src, lo, hi in ((big[a], 0, 256), (small[a], 256, T)):
+                nc.vector.quantize_mx(
+                    out=codes[a][:, lo:hi].bitcast(FP8X4),
+                    scales=plane[row:P, lo:hi],
+                    in_=src[:].rearrange("p w j -> p (w j)"),
+                )
+
+        def gather_words(a, lo, hi):
+            nc.vector.tensor_copy(
+                out=words[a][:, lo:hi], in_=codes[a][:].indirect(offs_list[:, lo // 16 : hi // 16])
+            )
+
+        def gather_bytes(lo, hi):
+            nc.vector.tensor_copy(
+                out=bytes_g[:, lo:hi], in_=planes[:].indirect(offs_list[:, lo // 16 : hi // 16])
+            )
+
+        def move_bytes(lo, hi):
+            for a in (4, 3):
+                nc.sync.dma_start(
+                    moved[a][0:MOVED_ROWS, lo:hi].bitcast(I32),
+                    bytes_g[ROW[a] : ROW[a] + MOVED_ROWS, lo:hi].bitcast(I32),
+                )
+
+        def grp(g):
+            return GROUP * g, GROUP * (g + 1)
+
+        nc.sync.dma_start(offs_list[:], offs)
+        load_x(4, 0, 256)
+        load_x(4, 256, T)
+        for a in (3, 2, 0, 1):
+            load_x(a, 0, T)
+
+        nc.vector.memset(planes_b[:].bitcast(I32), 0)
+        nc.vector.memset(planes[:, T:WINDOW].bitcast(I32), 0)
+        for a in range(PASSES):
+            nc.vector.memset(codes[a][:, T:WINDOW].bitcast(I32), 0)
+        load_scales(s8, w8_scales)
+
+        turn_all(4, big_v=True)
+        quantise(4)
+        nc.sync.dma_start(
+            planes[16 : 16 + MOVED_ROWS, 0:T].bitcast(I32), planes_b[12 : 12 + MOVED_ROWS, :].bitcast(I32)
+        )
+        load_scales(s4, w4_scales)
+        for g in range(GROUPS):
+            gather_words(4, *grp(g))
+        turn_all(3)
+        w = [load_weights(0, "slot_a")]
+        quantise(3)
+        gather_words(3, *grp(0))
+        gather_words(3, *grp(1))
+        turn_all(2)
+        w.append(load_weights(1, "slot_b"))
+        quantise(2)
+        turn_all(0, small_v=True)
+        gather_words(3, *grp(2))
+        turn_all(1, small_v=True)
+        gather_words(3, *grp(3))
+        quantise(0)
+        quantise(1)
+        for q in range(4):
+            rows = slice(32 * q, 32 * q + 16)
+            nc.vector.tensor_copy(out=planes[rows, 0:T].bitcast(I32), in_=planes_a[rows, :].bitcast(I32))
+        w.append(load_weights(2, "slot_c"))
+        for r, pos in enumerate((pos1, pos2, pos3, pos4)):
+            nc.sync.dma_start(pos_lists[r][:], pos)
+        gather_bytes(*grp(0))
+        gather_bytes(*grp(1))
+        move_bytes(0, 2 * GROUP)
+        gather_bytes(*grp(2))
+        gather_bytes(*grp(3))
+        move_bytes(2 * GROUP, SLOTS)
+        w.append(load_weights(3, "slot_d"))
+
+        def step(acc, e, h, a, col):
+            g, ee = divmod(e, W_EXPERTS)
+            w8, w4 = w[g]
+            ch = slice(P * h, P * (h + 1))
+            s = slice(C * e, C * (e + 1))
+            if a < PASSES8:
+                lhsT = w8[:, PASSES8 * ee + a, 4 * P * h : 4 * P * (h + 1)].bitcast(FP8X4)
+                lhsT_scale = s8[:, PASSES8 * e + a, ch]
+            else:
+                lhsT = w4[:, PASSES4 * ee + a - PASSES8, 2 * P * h : 2 * P * (h + 1)].bitcast(FP4X4)
+                lhsT_scale = s4[:, PASSES4 * e + a - PASSES8, ch]
+            rhs_scale = moved[a][:, s] if a in moved else bytes_g[ROW[a] : P, s]
+            nc.tensor.matmul_mx(
+                out=acc[:, C * col : C * (col + 1)],
+                lhsT=lhsT,
+                lhsT_scale=lhsT_scale,
+                rhs=words[a][:, s].bitcast(FP8X4),
+                rhs_scale=rhs_scale,
+                start=(a == SUM_ORDER[0]),
+                stop=(a == SUM_ORDER[-1]),
+            )
+
+        def run(experts):
+            accs = [psum.tile([P, WINDOW], F32, name="bank") for h in range(HALVES)]
+            for col, e in enumerate(experts):
+                for h in range(HALVES):
+                    for a in SUM_ORDER[:-1]:
+                        step(accs[h], e, h, a, col)
+                for h in range(HALVES):
+                    step(accs[h], e, h, SUM_ORDER[-1], col)
+            for h in range(HALVES):
+                nc.scalar.activation(
+                    y[h][:, C * experts[0] : C * (experts[-1] + 1)], accs[h][:, 0 : C * len(experts)], COPY
+                )
+
+        gates = []
+        for g in range(GROUPS):
+            lo, hi = grp(g)
+            gather_words(2, lo, hi)
+            gather_words(0, lo, hi)
+            first = W_EXPERTS * g
+            if g + 1 < GROUPS:
+                gather_words(1, lo, hi)
+                run((first, first + 1, first + 2))
+            else:
+                for s in range(lo, hi, C):
+                    gather_words(1, s, s + C)
+                run((first, first + 1))
+                run((first + 2,))
+            if g == 0:
+                gates = tile([P, HALVES * TOP, T], F32, "gates", "slot_a")
+                for h in range(HALVES):
+                    nc.sync.dma_start(
+                        gates[:, TOP * h : TOP * (h + 1), :],
+                        gate[:, P * h : P * (h + 1), :].rearrange("r p t -> p r t"),
+                    )
+
+        def fetch(h, r):
+            nc.vector.tensor_tensor(
+                prod[h][:, r, :], y[h][:].indirect(pos_lists[r][:]), gates[:, TOP * h + r, :], MULT
+            )
+
+        for h in range(HALVES):
+            fetch(h, 0)
+            fetch(h, 1)
+            fetch(h, 2)
+            nc.vector.tensor_tensor(part[h][:, 0, :], prod[h][:, 0, :], prod[h][:, 1, :], ADD)
+            fetch(h, 3)
+            nc.vector.tensor_tensor(part[h][:, 1, :], part[h][:, 0, :], prod[h][:, 2, :], ADD)
+            nc.vector.tensor_tensor(res[h][:], part[h][:, 1, :], prod[h][:, 3, :], ADD)
+            nc.sync.dma_start(out[P * h : P * (h + 1), :], res[h][:])

@@ -29,7 +29,7 @@ WINDOW = 512
 FLOPS = 2 * SLOTS * K * N
 
 ROW = {2: 0, 0: 4, 1: 8, 3: 12, 4: 16}
-SUM_ORDER = (2, 0, 4, 3, 1)
+CUTS = (0, 256, 512, 896, 1280, 1408, 1536)
 MOVED_ROWS = 112
 W8_BYTES = PASSES8 * 4 * N
 W4_BYTES = PASSES4 * 2 * N
@@ -53,8 +53,8 @@ def tile_moe_tk_lin_none_kernel(
         raw = [tile([P, 4, T], F32, "raw%d" % a, slot.get(a, "")) for a in range(PASSES)]
         big = [tile([P, 256, 4], BF16, "big%d" % a) for a in range(PASSES)]
         small = [tile([P, 128, 4], BF16, "small%d" % a) for a in range(PASSES)]
-        codes = [tile([P, WINDOW], U32, "codes%d" % a) for a in range(PASSES)]
-        words = [tile([P, SLOTS], U32, "words%d" % a) for a in range(PASSES)]
+        codes = [tile([P, WINDOW], U32, "codes%d" % a, "slot_e" if a == 2 else "") for a in range(PASSES)]
+        words = {a: tile([P, SLOTS], U32, "words%d" % a) for a in (2, 3, 4)}
         planes_a = tile([P, T], U8, "planes_a", "slot_c")
         planes_b = tile([P, T], U8, "planes_b")
         planes = tile([P, WINDOW], U8, "planes", "slot_d")
@@ -118,7 +118,7 @@ def tile_moe_tk_lin_none_kernel(
 
         def move_bytes(lo, hi):
             for a in (4, 3):
-                nc.sync.dma_start(
+                nc.scalar.dma_start(
                     moved[a][0:MOVED_ROWS, lo:hi].bitcast(I32),
                     bytes_g[ROW[a] : ROW[a] + MOVED_ROWS, lo:hi].bitcast(I32),
                 )
@@ -172,9 +172,15 @@ def tile_moe_tk_lin_none_kernel(
         gather_bytes(*grp(2))
         gather_bytes(*grp(3))
         move_bytes(2 * GROUP, SLOTS)
-        w.append(load_weights(3, "slot_d"))
+        late = tile([P, PASSES8, SLOTS], U32, "late_words", "slot_d")
+        words[0] = late[:, 0, :]
+        words[1] = late[:, 1, :]
+        for lo, hi in zip(CUTS, CUTS[1:]):
+            for a in (2, 0, 1):
+                gather_words(a, lo, hi)
+        w.append(load_weights(3, "slot_e"))
 
-        def step(acc, e, h, a, col):
+        def step(acc, e, h, a, col, first, last):
             g, ee = divmod(e, W_EXPERTS)
             w8, w4 = w[g]
             ch = slice(P * h, P * (h + 1))
@@ -192,44 +198,41 @@ def tile_moe_tk_lin_none_kernel(
                 lhsT_scale=lhsT_scale,
                 rhs=words[a][:, s].bitcast(FP8X4),
                 rhs_scale=rhs_scale,
-                start=(a == SUM_ORDER[0]),
-                stop=(a == SUM_ORDER[-1]),
+                start=first,
+                stop=last,
             )
 
-        def run(experts):
-            accs = [psum.tile([P, WINDOW], F32, name="bank") for h in range(HALVES)]
+        def bank():
+            return psum.tile([P, WINDOW], F32, name="bank")
+
+        def empty(acc, h, experts):
+            nc.scalar.activation(
+                y[h][:, C * experts[0] : C * (experts[-1] + 1)], acc[:, 0 : C * len(experts)], COPY
+            )
+
+        first_wave = [(e, h, bank()) for e in range(4) for h in range(HALVES)]
+        for passes in ((2, 0, 1), (4, 3)):
+            for e, h, acc in first_wave:
+                for a in passes:
+                    step(acc, e, h, a, 0, a == 2, a == 3)
+        for e, h, acc in first_wave:
+            empty(acc, h, (e,))
+        gates = tile([P, HALVES * TOP, T], F32, "gates", "slot_a")
+        for h in range(HALVES):
+            nc.sync.dma_start(
+                gates[:, TOP * h : TOP * (h + 1), :],
+                gate[:, P * h : P * (h + 1), :].rearrange("r p t -> p r t"),
+            )
+        for experts in ((4, 5, 6), (7, 8, 9), (10,), (11,)):
+            accs = [bank() for h in range(HALVES)]
             for col, e in enumerate(experts):
                 for h in range(HALVES):
-                    for a in SUM_ORDER[:-1]:
-                        step(accs[h], e, h, a, col)
+                    for a in (2, 0, 4, 3):
+                        step(accs[h], e, h, a, col, a == 2, False)
                 for h in range(HALVES):
-                    step(accs[h], e, h, SUM_ORDER[-1], col)
+                    step(accs[h], e, h, 1, col, False, True)
             for h in range(HALVES):
-                nc.scalar.activation(
-                    y[h][:, C * experts[0] : C * (experts[-1] + 1)], accs[h][:, 0 : C * len(experts)], COPY
-                )
-
-        gates = []
-        for g in range(GROUPS):
-            lo, hi = grp(g)
-            gather_words(2, lo, hi)
-            gather_words(0, lo, hi)
-            first = W_EXPERTS * g
-            if g + 1 < GROUPS:
-                gather_words(1, lo, hi)
-                run((first, first + 1, first + 2))
-            else:
-                for s in range(lo, hi, C):
-                    gather_words(1, s, s + C)
-                run((first, first + 1))
-                run((first + 2,))
-            if g == 0:
-                gates = tile([P, HALVES * TOP, T], F32, "gates", "slot_a")
-                for h in range(HALVES):
-                    nc.sync.dma_start(
-                        gates[:, TOP * h : TOP * (h + 1), :],
-                        gate[:, P * h : P * (h + 1), :].rearrange("r p t -> p r t"),
-                    )
+                empty(accs[h], h, experts)
 
         def fetch(h, r):
             nc.vector.tensor_tensor(

@@ -60,8 +60,6 @@ def tile_moe_tk_lin_none_kernel(
         planes = tile([P, WINDOW], U8, "planes", "slot_d")
         bytes_g = tile([P, SLOTS], U8, "bytes_g")
         moved = {a: tile([P, SLOTS], U8, "moved%d" % a) for a in (3, 4)}
-        s8 = tile([P, E * PASSES8, N], U8, "s8")
-        s4 = tile([P, E * PASSES4, N], U8, "s4")
         y = [tile([P, SLOTS], F32, "y%d" % h) for h in range(HALVES)]
         prod = [tile([P, TOP, T], F32, "prod%d" % h) for h in range(HALVES)]
         part = [tile([P, 2, T], F32, "part%d" % h) for h in range(HALVES)]
@@ -70,11 +68,6 @@ def tile_moe_tk_lin_none_kernel(
         def load_x(a, lo, hi):
             rows = xT[512 * a : 512 * (a + 1), :].rearrange("(p j) w -> p j w", j=4)
             nc.sync.dma_start(raw[a][:, :, lo:hi], rows[:, :, lo:hi])
-
-        def load_scales(scales, dram):
-            rows = dram.rearrange("e a (q r) n -> q r (e a) n", r=4)
-            for q in range(4):
-                nc.gpsimd.dma_start(scales[32 * q : 32 * q + 4, :, :].bitcast(I32), rows[q].bitcast(I32))
 
         def load_weights(g, slot_name):
             w = tile([P, W_EXPERTS * (W8_BYTES + W4_BYTES)], U8, "w%d" % g, slot_name)
@@ -129,21 +122,31 @@ def tile_moe_tk_lin_none_kernel(
         nc.sync.dma_start(offs_list[:], offs)
         load_x(4, 0, 256)
         load_x(4, 256, T)
-        for a in (3, 2, 0, 1):
+        for r, pos in enumerate((pos1, pos2, pos3, pos4)):
+            nc.sync.dma_start(pos_lists[r][:], pos)
+        load_x(3, 0, T)
+        n8 = E * PASSES8
+        stage = tile([16, E * PASSES, N], U8, "stage")
+        nc.sync.dma_start(stage[:, 0:n8, :].bitcast(I32), w8_scales.rearrange("e a q n -> q (e a) n").bitcast(I32))
+        nc.sync.dma_start(stage[:, n8:, :].bitcast(I32), w4_scales.rearrange("e a q n -> q (e a) n").bitcast(I32))
+        for a in (2, 0, 1):
             load_x(a, 0, T)
 
         nc.vector.memset(planes_b[:].bitcast(I32), 0)
         nc.vector.memset(planes[:, T:WINDOW].bitcast(I32), 0)
         for a in range(PASSES):
             nc.vector.memset(codes[a][:, T:WINDOW].bitcast(I32), 0)
-        load_scales(s8, w8_scales)
 
         turn_all(4, big_v=True)
         quantise(4)
-        nc.sync.dma_start(
+        nc.scalar.dma_start(
             planes[16 : 16 + MOVED_ROWS, 0:T].bitcast(I32), planes_b[12 : 12 + MOVED_ROWS, :].bitcast(I32)
         )
-        load_scales(s4, w4_scales)
+        scales = tile([P, E * PASSES, N], U8, "scales")
+        for q in range(4):
+            nc.sync.dma_start(
+                scales[32 * q : 32 * q + 4, :, :].bitcast(I32), stage[4 * q : 4 * q + 4, :, :].bitcast(I32)
+            )
         for g in range(GROUPS):
             gather_words(4, *grp(g))
         turn_all(3)
@@ -163,16 +166,14 @@ def tile_moe_tk_lin_none_kernel(
         for q in range(4):
             rows = slice(32 * q, 32 * q + 16)
             nc.vector.tensor_copy(out=planes[rows, 0:T].bitcast(I32), in_=planes_a[rows, :].bitcast(I32))
-        w.append(load_weights(2, "slot_c"))
-        for r, pos in enumerate((pos1, pos2, pos3, pos4)):
-            nc.sync.dma_start(pos_lists[r][:], pos)
         gather_bytes(*grp(0))
         gather_bytes(*grp(1))
         move_bytes(0, 2 * GROUP)
         gather_bytes(*grp(2))
         gather_bytes(*grp(3))
         move_bytes(2 * GROUP, SLOTS)
-        late = tile([P, PASSES8, SLOTS], U32, "late_words", "slot_d")
+        w.append(load_weights(2, "slot_d"))
+        late = tile([P, PASSES8, SLOTS], U32, "late_words", "slot_c")
         words[0] = late[:, 0, :]
         words[1] = late[:, 1, :]
         for lo, hi in zip(CUTS, CUTS[1:]):
@@ -187,10 +188,10 @@ def tile_moe_tk_lin_none_kernel(
             s = slice(C * e, C * (e + 1))
             if a < PASSES8:
                 lhsT = w8[:, PASSES8 * ee + a, 4 * P * h : 4 * P * (h + 1)].bitcast(FP8X4)
-                lhsT_scale = s8[:, PASSES8 * e + a, ch]
+                lhsT_scale = scales[:, PASSES8 * e + a, ch]
             else:
                 lhsT = w4[:, PASSES4 * ee + a - PASSES8, 2 * P * h : 2 * P * (h + 1)].bitcast(FP4X4)
-                lhsT_scale = s4[:, PASSES4 * e + a - PASSES8, ch]
+                lhsT_scale = scales[:, n8 + PASSES4 * e + a - PASSES8, ch]
             rhs_scale = moved[a][:, s] if a in moved else bytes_g[ROW[a] : P, s]
             nc.tensor.matmul_mx(
                 out=acc[:, C * col : C * (col + 1)],
@@ -223,16 +224,13 @@ def tile_moe_tk_lin_none_kernel(
                 gates[:, TOP * h : TOP * (h + 1), :],
                 gate[:, P * h : P * (h + 1), :].rearrange("r p t -> p r t"),
             )
-        for experts in ((4, 5, 6), (7, 8, 9), (10,), (11,)):
-            accs = [bank() for h in range(HALVES)]
-            for col, e in enumerate(experts):
-                for h in range(HALVES):
-                    for a in (2, 0, 4, 3):
-                        step(accs[h], e, h, a, col, a == 2, False)
-                for h in range(HALVES):
-                    step(accs[h], e, h, 1, col, False, True)
-            for h in range(HALVES):
-                empty(accs[h], h, experts)
+        for h in range(HALVES):
+            for experts in ((4, 5, 6), (7, 8, 9), (10,), (11,)):
+                acc = bank()
+                for col, e in enumerate(experts):
+                    for a in (2, 0, 4, 3, 1):
+                        step(acc, e, h, a, col, a == 2, a == 1)
+                empty(acc, h, experts)
 
         def fetch(h, r):
             nc.vector.tensor_tensor(

@@ -28,11 +28,9 @@ W_EXPERTS = E // GROUPS
 WINDOW = 512
 FLOPS = 2 * SLOTS * K * N
 
-ROW = {2: 0, 0: 4, 1: 8, 3: 12, 4: 16}
+PLANES = 3
+PLACE = {2: (0, 0), 0: (0, 4), 1: (0, 8), 3: (1, 0), 4: (2, 0)}
 CUTS = (0, 256, 512, 896, 1280, 1408, 1536)
-MOVED_ROWS = 112
-W8_BYTES = PASSES8 * 4 * N
-W4_BYTES = PASSES4 * 2 * N
 
 
 def tile_moe_tk_lin_none_kernel(
@@ -49,17 +47,18 @@ def tile_moe_tk_lin_none_kernel(
         offs_list = keep.tile([P, SLOTS // 16], U16, name="offs_list")
         pos_lists = [keep.tile([P, T // 16], U16, name="pos%d_list" % r) for r in range(TOP)]
 
-        slot = {3: "slot_a", 2: "slot_b"}
-        raw = [tile([P, 4, T], F32, "raw%d" % a, slot.get(a, "")) for a in range(PASSES)]
+        raw = [tile([P, 4, T], F32, "raw%d" % a) for a in range(PASSES)]
         big = [tile([P, 256, 4], BF16, "big%d" % a) for a in range(PASSES)]
         small = [tile([P, 128, 4], BF16, "small%d" % a) for a in range(PASSES)]
-        codes = [tile([P, WINDOW], U32, "codes%d" % a, "slot_e" if a == 2 else "") for a in range(PASSES)]
-        words = {a: tile([P, SLOTS], U32, "words%d" % a) for a in (2, 3, 4)}
-        planes_a = tile([P, T], U8, "planes_a", "slot_c")
-        planes_b = tile([P, T], U8, "planes_b")
-        planes = tile([P, WINDOW], U8, "planes", "slot_d")
-        bytes_g = tile([P, SLOTS], U8, "bytes_g")
-        moved = {a: tile([P, SLOTS], U8, "moved%d" % a) for a in (3, 4)}
+        codes = [tile([P, WINDOW], U32, "codes%d" % a) for a in range(PASSES)]
+        words = [tile([P, SLOTS], U32, "words%d" % a) for a in range(PASSES)]
+        planes = [tile([P, WINDOW], U8, "planes%d" % i) for i in range(PLANES)]
+        bytes_g = [tile([P, SLOTS], U8, "bytes%d" % i) for i in range(PLANES)]
+        stage = tile([16, E * PASSES, N], U8, "stage")
+        scales = tile([P, E * PASSES, N], U8, "scales")
+        w8 = [tile([P, W_EXPERTS * PASSES8, 4 * N], U8, "w8_%d" % g) for g in range(GROUPS)]
+        w4 = [tile([P, W_EXPERTS * PASSES4, 2 * N], U8, "w4_%d" % g) for g in range(GROUPS)]
+        gates = [tile([P, TOP, T], F32, "gates%d" % h) for h in range(HALVES)]
         y = [tile([P, SLOTS], F32, "y%d" % h) for h in range(HALVES)]
         prod = [tile([P, TOP, T], F32, "prod%d" % h) for h in range(HALVES)]
         part = [tile([P, 2, T], F32, "part%d" % h) for h in range(HALVES)]
@@ -69,33 +68,19 @@ def tile_moe_tk_lin_none_kernel(
             rows = xT[512 * a : 512 * (a + 1), :].rearrange("(p j) w -> p j w", j=4)
             nc.sync.dma_start(raw[a][:, :, lo:hi], rows[:, :, lo:hi])
 
-        def load_weights(g, slot_name):
-            w = tile([P, W_EXPERTS * (W8_BYTES + W4_BYTES)], U8, "w%d" % g, slot_name)
-            ee = slice(W_EXPERTS * g, W_EXPERTS * (g + 1))
-            w8 = w[:, 0 : W_EXPERTS * W8_BYTES].rearrange("p (ea b) -> p ea b", b=4 * N)
-            w4 = w[:, W_EXPERTS * W8_BYTES :].rearrange("p (ea b) -> p ea b", b=2 * N)
-            nc.sync.dma_start(w8.bitcast(I32), w8_words[ee].rearrange("e a p n r -> p (e a) (n r)").bitcast(I32))
-            nc.sync.dma_start(w4.bitcast(I32), w4_words[ee].rearrange("e a p b -> p (e a) b").bitcast(I32))
-            return w8, w4
-
-        def turn(dst, a, lo, hi, on_vector):
+        def turn(dst, a, lo, hi, on_vector=False):
             src = raw[a][:, :, lo:hi].rearrange("p j w -> p w j")
             if on_vector:
                 nc.vector.tensor_copy(out=dst[:], in_=src)
             else:
                 nc.scalar.activation(dst[:], src, COPY)
 
-        def turn_all(a, big_v=False, small_v=False):
-            turn(big[a], a, 0, 256, big_v)
-            turn(small[a], a, 256, T, small_v)
-
         def quantise(a):
-            row = min(ROW[a], 12)
-            plane = planes_b if a == 4 else planes_a
+            i, row = PLACE[a]
             for src, lo, hi in ((big[a], 0, 256), (small[a], 256, T)):
                 nc.vector.quantize_mx(
                     out=codes[a][:, lo:hi].bitcast(FP8X4),
-                    scales=plane[row:P, lo:hi],
+                    scales=planes[i][row:P, lo:hi],
                     in_=src[:].rearrange("p w j -> p (w j)"),
                 )
 
@@ -104,101 +89,76 @@ def tile_moe_tk_lin_none_kernel(
                 out=words[a][:, lo:hi], in_=codes[a][:].indirect(offs_list[:, lo // 16 : hi // 16])
             )
 
-        def gather_bytes(lo, hi):
+        def gather_bytes(i, lo, hi):
             nc.vector.tensor_copy(
-                out=bytes_g[:, lo:hi], in_=planes[:].indirect(offs_list[:, lo // 16 : hi // 16])
+                out=bytes_g[i][:, lo:hi], in_=planes[i][:].indirect(offs_list[:, lo // 16 : hi // 16])
             )
-
-        def move_bytes(lo, hi):
-            for a in (4, 3):
-                nc.scalar.dma_start(
-                    moved[a][0:MOVED_ROWS, lo:hi].bitcast(I32),
-                    bytes_g[ROW[a] : ROW[a] + MOVED_ROWS, lo:hi].bitcast(I32),
-                )
-
-        def grp(g):
-            return GROUP * g, GROUP * (g + 1)
 
         nc.sync.dma_start(offs_list[:], offs)
         load_x(4, 0, 256)
         load_x(4, 256, T)
-        for r, pos in enumerate((pos1, pos2, pos3, pos4)):
-            nc.sync.dma_start(pos_lists[r][:], pos)
         load_x(3, 0, T)
         n8 = E * PASSES8
-        stage = tile([16, E * PASSES, N], U8, "stage")
         nc.sync.dma_start(stage[:, 0:n8, :].bitcast(I32), w8_scales.rearrange("e a q n -> q (e a) n").bitcast(I32))
         nc.sync.dma_start(stage[:, n8:, :].bitcast(I32), w4_scales.rearrange("e a q n -> q (e a) n").bitcast(I32))
         for a in (2, 0, 1):
             load_x(a, 0, T)
-
-        nc.vector.memset(planes_b[:].bitcast(I32), 0)
-        nc.vector.memset(planes[:, T:WINDOW].bitcast(I32), 0)
-        for a in range(PASSES):
-            nc.vector.memset(codes[a][:, T:WINDOW].bitcast(I32), 0)
-
-        turn_all(4, big_v=True)
-        quantise(4)
-        nc.scalar.dma_start(
-            planes[16 : 16 + MOVED_ROWS, 0:T].bitcast(I32), planes_b[12 : 12 + MOVED_ROWS, :].bitcast(I32)
-        )
-        scales = tile([P, E * PASSES, N], U8, "scales")
         for q in range(4):
             nc.sync.dma_start(
                 scales[32 * q : 32 * q + 4, :, :].bitcast(I32), stage[4 * q : 4 * q + 4, :, :].bitcast(I32)
             )
         for g in range(GROUPS):
-            gather_words(4, *grp(g))
-        turn_all(3)
-        w = [load_weights(0, "slot_a")]
-        quantise(3)
-        gather_words(3, *grp(0))
-        gather_words(3, *grp(1))
-        turn_all(2)
-        w.append(load_weights(1, "slot_b"))
-        quantise(2)
-        turn_all(0, small_v=True)
-        gather_words(3, *grp(2))
-        turn_all(1, small_v=True)
-        gather_words(3, *grp(3))
+            ee = slice(W_EXPERTS * g, W_EXPERTS * (g + 1))
+            nc.sync.dma_start(
+                w8[g][:].bitcast(I32), w8_words[ee].rearrange("e a p n r -> p (e a) (n r)").bitcast(I32)
+            )
+            nc.sync.dma_start(w4[g][:].bitcast(I32), w4_words[ee].rearrange("e a p b -> p (e a) b").bitcast(I32))
+        for r, pos in enumerate((pos1, pos2, pos3, pos4)):
+            nc.sync.dma_start(pos_lists[r][:], pos)
+        for h in range(HALVES):
+            nc.sync.dma_start(gates[h][:], gate[:, P * h : P * (h + 1), :].rearrange("r p t -> p r t"))
+
+        for t in planes:
+            nc.vector.memset(t[:].bitcast(I32), 0)
+        for a in (4, 3, 2, 0, 1):
+            nc.vector.memset(codes[a][:, T:WINDOW].bitcast(I32), 0)
+
+        turn(big[4], 4, 0, 256, on_vector=True)
+        turn(small[4], 4, 256, T)
+        for a in (3, 2, 0, 1):
+            turn(big[a], a, 0, 256)
+            turn(small[a], a, 256, T)
+        for a in (4, 3, 2):
+            quantise(a)
+            for lo in range(0, SLOTS, GROUP):
+                gather_words(a, lo, lo + GROUP)
+            if a != 2:
+                for lo in range(0, SLOTS, GROUP):
+                    gather_bytes(PLACE[a][0], lo, lo + GROUP)
         quantise(0)
         quantise(1)
-        for q in range(4):
-            rows = slice(32 * q, 32 * q + 16)
-            nc.vector.tensor_copy(out=planes[rows, 0:T].bitcast(I32), in_=planes_a[rows, :].bitcast(I32))
-        gather_bytes(*grp(0))
-        gather_bytes(*grp(1))
-        move_bytes(0, 2 * GROUP)
-        gather_bytes(*grp(2))
-        gather_bytes(*grp(3))
-        move_bytes(2 * GROUP, SLOTS)
-        w.append(load_weights(2, "slot_d"))
-        late = tile([P, PASSES8, SLOTS], U32, "late_words", "slot_c")
-        words[0] = late[:, 0, :]
-        words[1] = late[:, 1, :]
         for lo, hi in zip(CUTS, CUTS[1:]):
-            for a in (2, 0, 1):
-                gather_words(a, lo, hi)
-        w.append(load_weights(3, "slot_e"))
+            gather_bytes(0, lo, hi)
+            gather_words(0, lo, hi)
+            gather_words(1, lo, hi)
 
         def step(acc, e, h, a, col, first, last):
             g, ee = divmod(e, W_EXPERTS)
-            w8, w4 = w[g]
             ch = slice(P * h, P * (h + 1))
             s = slice(C * e, C * (e + 1))
             if a < PASSES8:
-                lhsT = w8[:, PASSES8 * ee + a, 4 * P * h : 4 * P * (h + 1)].bitcast(FP8X4)
+                lhsT = w8[g][:, PASSES8 * ee + a, 4 * P * h : 4 * P * (h + 1)].bitcast(FP8X4)
                 lhsT_scale = scales[:, PASSES8 * e + a, ch]
             else:
-                lhsT = w4[:, PASSES4 * ee + a - PASSES8, 2 * P * h : 2 * P * (h + 1)].bitcast(FP4X4)
+                lhsT = w4[g][:, PASSES4 * ee + a - PASSES8, 2 * P * h : 2 * P * (h + 1)].bitcast(FP4X4)
                 lhsT_scale = scales[:, n8 + PASSES4 * e + a - PASSES8, ch]
-            rhs_scale = moved[a][:, s] if a in moved else bytes_g[ROW[a] : P, s]
+            i, row = PLACE[a]
             nc.tensor.matmul_mx(
                 out=acc[:, C * col : C * (col + 1)],
                 lhsT=lhsT,
                 lhsT_scale=lhsT_scale,
                 rhs=words[a][:, s].bitcast(FP8X4),
-                rhs_scale=rhs_scale,
+                rhs_scale=bytes_g[i][row:P, s],
                 start=first,
                 stop=last,
             )
@@ -212,29 +172,24 @@ def tile_moe_tk_lin_none_kernel(
             )
 
         first_wave = [(e, h, bank()) for e in range(4) for h in range(HALVES)]
-        for passes in ((2, 0, 1), (4, 3)):
-            for e, h, acc in first_wave:
-                for a in passes:
-                    step(acc, e, h, a, 0, a == 2, a == 3)
         for e, h, acc in first_wave:
+            for a in (4, 3):
+                step(acc, e, h, a, 0, a == 4, False)
+        for e, h, acc in first_wave:
+            for a in (2, 0, 1):
+                step(acc, e, h, a, 0, False, a == 1)
             empty(acc, h, (e,))
-        gates = tile([P, HALVES * TOP, T], F32, "gates", "slot_a")
-        for h in range(HALVES):
-            nc.sync.dma_start(
-                gates[:, TOP * h : TOP * (h + 1), :],
-                gate[:, P * h : P * (h + 1), :].rearrange("r p t -> p r t"),
-            )
         for h in range(HALVES):
             for experts in ((4, 5, 6), (7, 8, 9), (10,), (11,)):
                 acc = bank()
                 for col, e in enumerate(experts):
-                    for a in (2, 0, 4, 3, 1):
-                        step(acc, e, h, a, col, a == 2, a == 1)
+                    for a in (4, 3, 2, 0, 1):
+                        step(acc, e, h, a, col, a == 4, a == 1)
                 empty(acc, h, experts)
 
         def fetch(h, r):
             nc.vector.tensor_tensor(
-                prod[h][:, r, :], y[h][:].indirect(pos_lists[r][:]), gates[:, TOP * h + r, :], MULT
+                prod[h][:, r, :], y[h][:].indirect(pos_lists[r][:]), gates[h][:, r, :], MULT
             )
 
         for h in range(HALVES):

from contextlib import ExitStack

import concourse.mybir as mybir

F32 = mybir.dt.float32
BF16 = mybir.dt.bfloat16
I32 = mybir.dt.int32
U32 = mybir.dt.uint32
U16 = mybir.dt.uint16
U8 = mybir.dt.uint8
FP8X4 = mybir.dt.float8_e4m3fn_x4
FP4X4 = mybir.dt.float4_e2m1fn_x4
COPY = mybir.ActivationFunctionType.Copy
MULT = mybir.AluOpType.mult
ADD = mybir.AluOpType.add

P = 128
K, T, E, C, N = 2560, 384, 12, 128, 256
TOP = 4
SLOTS = E * C
PASSES = 5
PASSES8 = 2
PASSES4 = 3
HALVES = N // P
GROUP = 384
GROUPS = SLOTS // GROUP
W_EXPERTS = E // GROUPS
WINDOW = 512
FLOPS = 2 * SLOTS * K * N

PLANES = 3
PLACE = {2: (0, 0), 0: (0, 4), 1: (0, 8), 3: (1, 0), 4: (2, 0)}
CUTS = (0, 256, 512, 896, 1280, 1408, 1536)


def tile_moe_tk_lin_none_kernel(
    tc, xT, w8_words, w8_scales, w4_words, w4_scales, gate, offs, pos1, pos2, pos3, pos4, out
):
    nc = tc.nc
    with ExitStack() as ctx:
        keep = ctx.enter_context(tc.tile_pool(name="keep", bufs=1))
        psum = ctx.enter_context(tc.psum_pool(name="psum", bufs=8))

        def tile(shape, dtype, name, tag=""):
            return keep.tile(shape, dtype, name=name, tag=tag or name, align_bytes=64)

        offs_list = keep.tile([P, SLOTS // 16], U16, name="offs_list")
        pos_lists = [keep.tile([P, T // 16], U16, name="pos%d_list" % r) for r in range(TOP)]

        raw = [tile([P, 4, T], F32, "raw%d" % a) for a in range(PASSES)]
        big = [tile([P, 256, 4], BF16, "big%d" % a) for a in range(PASSES)]
        small = [tile([P, 128, 4], BF16, "small%d" % a) for a in range(PASSES)]
        codes = [tile([P, WINDOW], U32, "codes%d" % a) for a in range(PASSES)]
        words = [tile([P, SLOTS], U32, "words%d" % a) for a in range(PASSES)]
        planes = [tile([P, WINDOW], U8, "planes%d" % i) for i in range(PLANES)]
        bytes_g = [tile([P, SLOTS], U8, "bytes%d" % i) for i in range(PLANES)]
        stage = tile([16, E * PASSES, N], U8, "stage")
        scales = tile([P, E * PASSES, N], U8, "scales")
        w8 = [tile([P, W_EXPERTS * PASSES8, 4 * N], U8, "w8_%d" % g) for g in range(GROUPS)]
        w4 = [tile([P, W_EXPERTS * PASSES4, 2 * N], U8, "w4_%d" % g) for g in range(GROUPS)]
        gates = [tile([P, TOP, T], F32, "gates%d" % h) for h in range(HALVES)]
        y = [tile([P, SLOTS], F32, "y%d" % h) for h in range(HALVES)]
        prod = [tile([P, TOP, T], F32, "prod%d" % h) for h in range(HALVES)]
        part = [tile([P, 2, T], F32, "part%d" % h) for h in range(HALVES)]
        res = [tile([P, T], F32, "res%d" % h) for h in range(HALVES)]

        def load_x(a, lo, hi):
            rows = xT[512 * a : 512 * (a + 1), :].rearrange("(p j) w -> p j w", j=4)
            nc.sync.dma_start(raw[a][:, :, lo:hi], rows[:, :, lo:hi])

        def turn(dst, a, lo, hi, on_vector=False):
            src = raw[a][:, :, lo:hi].rearrange("p j w -> p w j")
            if on_vector:
                nc.vector.tensor_copy(out=dst[:], in_=src)
            else:
                nc.scalar.activation(dst[:], src, COPY)

        def quantise(a):
            i, row = PLACE[a]
            for src, lo, hi in ((big[a], 0, 256), (small[a], 256, T)):
                nc.vector.quantize_mx(
                    out=codes[a][:, lo:hi].bitcast(FP8X4),
                    scales=planes[i][row:P, lo:hi],
                    in_=src[:].rearrange("p w j -> p (w j)"),
                )

        def gather_words(a, lo, hi):
            nc.vector.tensor_copy(
                out=words[a][:, lo:hi], in_=codes[a][:].indirect(offs_list[:, lo // 16 : hi // 16])
            )

        def gather_bytes(i, lo, hi):
            nc.vector.tensor_copy(
                out=bytes_g[i][:, lo:hi], in_=planes[i][:].indirect(offs_list[:, lo // 16 : hi // 16])
            )

        nc.sync.dma_start(offs_list[:], offs)
        load_x(4, 0, 256)
        load_x(4, 256, T)
        load_x(3, 0, T)
        n8 = E * PASSES8
        nc.sync.dma_start(stage[:, 0:n8, :].bitcast(I32), w8_scales.rearrange("e a q n -> q (e a) n").bitcast(I32))
        nc.sync.dma_start(stage[:, n8:, :].bitcast(I32), w4_scales.rearrange("e a q n -> q (e a) n").bitcast(I32))
        for a in (2, 0, 1):
            load_x(a, 0, T)
        for q in range(4):
            nc.sync.dma_start(
                scales[32 * q : 32 * q + 4, :, :].bitcast(I32), stage[4 * q : 4 * q + 4, :, :].bitcast(I32)
            )
        for g in range(GROUPS):
            ee = slice(W_EXPERTS * g, W_EXPERTS * (g + 1))
            nc.sync.dma_start(
                w8[g][:].bitcast(I32), w8_words[ee].rearrange("e a p n r -> p (e a) (n r)").bitcast(I32)
            )
            nc.sync.dma_start(w4[g][:].bitcast(I32), w4_words[ee].rearrange("e a p b -> p (e a) b").bitcast(I32))
        for r, pos in enumerate((pos1, pos2, pos3, pos4)):
            nc.sync.dma_start(pos_lists[r][:], pos)
        for h in range(HALVES):
            nc.sync.dma_start(gates[h][:], gate[:, P * h : P * (h + 1), :].rearrange("r p t -> p r t"))

        for t in planes:
            nc.vector.memset(t[:].bitcast(I32), 0)
        for a in (4, 3, 2, 0, 1):
            nc.vector.memset(codes[a][:, T:WINDOW].bitcast(I32), 0)

        turn(big[4], 4, 0, 256, on_vector=True)
        turn(small[4], 4, 256, T)
        for a in (3, 2, 0, 1):
            turn(big[a], a, 0, 256)
            turn(small[a], a, 256, T)
        for a in (4, 3, 2):
            quantise(a)
            for lo in range(0, SLOTS, GROUP):
                gather_words(a, lo, lo + GROUP)
            if a != 2:
                for lo in range(0, SLOTS, GROUP):
                    gather_bytes(PLACE[a][0], lo, lo + GROUP)
        quantise(0)
        quantise(1)
        for lo, hi in zip(CUTS, CUTS[1:]):
            gather_bytes(0, lo, hi)
            gather_words(0, lo, hi)
            gather_words(1, lo, hi)

        def step(acc, e, h, a, col, first, last):
            g, ee = divmod(e, W_EXPERTS)
            ch = slice(P * h, P * (h + 1))
            s = slice(C * e, C * (e + 1))
            if a < PASSES8:
                lhsT = w8[g][:, PASSES8 * ee + a, 4 * P * h : 4 * P * (h + 1)].bitcast(FP8X4)
                lhsT_scale = scales[:, PASSES8 * e + a, ch]
            else:
                lhsT = w4[g][:, PASSES4 * ee + a - PASSES8, 2 * P * h : 2 * P * (h + 1)].bitcast(FP4X4)
                lhsT_scale = scales[:, n8 + PASSES4 * e + a - PASSES8, ch]
            i, row = PLACE[a]
            nc.tensor.matmul_mx(
                out=acc[:, C * col : C * (col + 1)],
                lhsT=lhsT,
                lhsT_scale=lhsT_scale,
                rhs=words[a][:, s].bitcast(FP8X4),
                rhs_scale=bytes_g[i][row:P, s],
                start=first,
                stop=last,
            )

        def bank():
            return psum.tile([P, WINDOW], F32, name="bank")

        def empty(acc, h, experts):
            nc.scalar.activation(
                y[h][:, C * experts[0] : C * (experts[-1] + 1)], acc[:, 0 : C * len(experts)], COPY
            )

        first_wave = [(e, h, bank()) for e in range(4) for h in range(HALVES)]
        for e, h, acc in first_wave:
            for a in (4, 3):
                step(acc, e, h, a, 0, a == 4, False)
        for e, h, acc in first_wave:
            for a in (2, 0, 1):
                step(acc, e, h, a, 0, False, a == 1)
            empty(acc, h, (e,))
        for h in range(HALVES):
            for experts in ((4, 5, 6), (7, 8, 9), (10,), (11,)):
                acc = bank()
                for col, e in enumerate(experts):
                    for a in (4, 3, 2, 0, 1):
                        step(acc, e, h, a, col, a == 4, a == 1)
                empty(acc, h, experts)

        def fetch(h, r):
            nc.vector.tensor_tensor(
                prod[h][:, r, :], y[h][:].indirect(pos_lists[r][:]), gates[h][:, r, :], MULT
            )

        for h in range(HALVES):
            fetch(h, 0)
            fetch(h, 1)
            fetch(h, 2)
            nc.vector.tensor_tensor(part[h][:, 0, :], prod[h][:, 0, :], prod[h][:, 1, :], ADD)
            fetch(h, 3)
            nc.vector.tensor_tensor(part[h][:, 1, :], part[h][:, 0, :], prod[h][:, 2, :], ADD)
            nc.vector.tensor_tensor(res[h][:], part[h][:, 1, :], prod[h][:, 3, :], ADD)
            nc.sync.dma_start(out[P * h : P * (h + 1), :], res[h][:])
